import numpy as np
import ml_dtypes


def mxq(x, axis, fmt="e4m3"):
    dtype, down = {"e4m3": (ml_dtypes.float8_e4m3fn, 7), "e5m2": (ml_dtypes.float8_e5m2, 14)}[fmt]
    v = np.moveaxis(np.asarray(x, np.float32).astype(ml_dtypes.bfloat16).astype(np.float64), axis, -1)
    blocks = v.reshape(v.shape[:-1] + (-1, 32))
    amax = np.abs(blocks).max(-1, keepdims=True)
    byte = np.maximum(np.where(amax > 0, np.frexp(amax)[1] - 1 + 127, 0) - down, 1)
    scale = np.exp2(byte - 127.0)
    codes = (blocks / scale).astype(np.float32).astype(dtype).astype(np.float64)
    return np.moveaxis((codes * scale).reshape(v.shape), -1, axis)


WIDE = False


def mx_kscale(k):
    if not WIDE:
        return np.ones(k)
    levels = np.array([10, -10, 5, -5, 0])
    if k % 512:
        return np.exp2(np.random.permutation(np.resize(levels, k // 32))).repeat(32)
    a = np.empty((k // 512, 16))
    for p in range(k // 512):
        a[p, :8] = np.random.permutation(np.resize(levels, 8))
        for g in range(8):
            far = levels[np.abs(levels - a[p, g]) >= 10]
            a[p, g + 8] = far[np.random.randint(len(far))]
    return np.exp2(a.ravel()).repeat(32)


def f64(x):
    return np.asarray(x).astype(np.float64)


def striped(idx):
    return np.tile(idx.reshape(-1, 16).T, (8, 1)).astype(np.uint16)


def unstriped(offs):
    return offs[:16].T.reshape(-1).astype(np.int64)


K, T, D, S, V, N = 1024, 1024, 8, 4096, 512, 256


def setup_inputs():
    n = np.random.standard_normal
    s = mx_kscale(K)[:, None]
    return {
        "xT": (n((K, T)) * s).astype(np.float32),
        "w": (n((K, N)) / np.sqrt(K) / s).astype(np.float32),
        "offs": striped(np.concatenate([np.random.permutation(T)[:V] for _ in range(D)])),
    }


def reference(xT, w, offs):
    idx = unstriped(offs)
    x = np.empty((K, V))
    for l in range(D):
        r = l // 4 * (4 * K // D) + l % 4 + 4 * np.arange(K // D)
        x[r] = f64(xT)[r][:, idx[l * V:(l + 1) * V]]
    xq = mxq(x, 0, "e4m3")
    return mxq(f64(w), 0, "e4m3").T @ xq

@@ -1,0 +1,175 @@
+from contextlib import ExitStack
+
+import concourse.mybir as mybir
+
+K, T, D, V, N = 1024, 1024, 8, 512, 256
+FLOPS = 2 * K * N * V
+
+F32 = mybir.dt.float32
+BF16 = mybir.dt.bfloat16
+U32 = mybir.dt.uint32
+U16 = mybir.dt.uint16
+U8 = mybir.dt.uint8
+FP8X4 = mybir.dt.float8_e4m3fn_x4
+
+COPY = mybir.ActivationFunctionType.Copy
+
+P = 128
+PACK = 4
+K_PASS = P * PACK
+PASSES = K // K_PASS
+HALF = V // 2
+
+
+def tile_picked_grid_lin_none_sub_l_kernel(tc, xT, w, offs, out):
+    nc = tc.nc
+    with ExitStack() as ctx:
+        keep = ctx.enter_context(tc.tile_pool(name="keep", bufs=1))
+        psum = ctx.enter_context(tc.psum_pool(name="psum", bufs=1))
+
+        offsets = keep.tile([P, D * V // 16], U16, name="offsets")
+        nc.sync.dma_start(offsets[:], offs)
+
+        warm = keep.tile([P, 1], F32, name="warm")
+        warm_out = keep.tile([P, 1], F32, name="warm_out")
+        nc.vector.memset(warm[:], 0.0)
+        nc.scalar.activation(warm_out[:], warm[:], COPY)
+
+        tables = {}
+        w_raw = []
+
+        def load_level(l):
+            g, j = divmod(l, PACK)
+            table = keep.tile([P, T], F32, name=f"table{l}", align_bytes=64)
+            rows = xT[g * K_PASS : (g + 1) * K_PASS, :].rearrange("(p j) t -> p j t", j=PACK)
+            nc.sync.dma_start(out=table[:], in_=rows[:, j, :])
+            tables[l] = table
+
+        def load_w(g):
+            raw = keep.tile([P, PACK, N], F32, name=f"w_raw{g}", align_bytes=64)
+            nc.sync.dma_start(out=raw[:], in_=w[g * K_PASS : (g + 1) * K_PASS, :].rearrange("(p j) n -> p j n", j=PACK))
+            w_raw.append(raw)
+
+        load_level(0)
+        load_level(2)
+        load_level(1)
+        load_level(3)
+        load_w(0)
+        load_w(1)
+        load_level(4)
+        load_level(5)
+        load_level(6)
+        load_level(7)
+
+        picked = [keep.tile([P, PACK, V], F32, name=f"picked{g}", align_bytes=64) for g in range(PASSES)]
+        grouped = [keep.tile([P, V, PACK], BF16, name=f"grouped{g}", align_bytes=64) for g in range(PASSES)]
+        codes = [keep.tile([P, V], U32, name=f"codes{g}", align_bytes=64) for g in range(PASSES)]
+        scales = [keep.tile([P, V], U8, name=f"scales{g}", align_bytes=64) for g in range(PASSES)]
+        w_grouped = [keep.tile([P, N, PACK], BF16, name=f"w_grouped{g}", align_bytes=64) for g in range(PASSES)]
+        w_codes = [keep.tile([P, N], U32, name=f"w_codes{g}", align_bytes=64) for g in range(PASSES)]
+        w_scales = [keep.tile([P, N], U8, name=f"w_scales{g}", align_bytes=64) for g in range(PASSES)]
+        acc = [[psum.tile([P, HALF], F32, name=f"acc{m}{c}") for c in range(2)] for m in range(2)]
+        res = [[keep.tile([P, HALF], F32, name=f"res{m}{c}", align_bytes=64) for c in range(2)] for m in range(2)]
+
+        def gather(l, v0, v1):
+            g, j = divmod(l, PACK)
+            c0 = l * V // 16
+            nc.vector.tensor_copy(
+                picked[g][:, j, v0:v1],
+                tables[l][:].indirect(offsets[:, c0 + v0 // 16 : c0 + v1 // 16]),
+            )
+
+        def interleave(copy, g, j0, j1, v0, v1):
+            copy(
+                out=grouped[g][:, v0:v1, j0:j1],
+                in_=picked[g][:, j0:j1, v0:v1].rearrange("p j v -> p v j"),
+            )
+
+        def quantize(g, v0, v1):
+            nc.vector.quantize_mx(
+                out=codes[g][:, v0:v1].bitcast(FP8X4),
+                scales=scales[g][:, v0:v1],
+                in_=grouped[g][:, v0:v1, :].rearrange("p v j -> p (v j)"),
+            )
+
+        def interleave_w(copy, g):
+            copy(out=w_grouped[g][:], in_=w_raw[g][:].rearrange("p j n -> p n j"))
+
+        def quantize_w(g):
+            nc.vector.quantize_mx(
+                out=w_codes[g][:].bitcast(FP8X4),
+                scales=w_scales[g][:],
+                in_=w_grouped[g][:].rearrange("p n j -> p (n j)"),
+            )
+
+        def multiply(g, m, c):
+            mc = slice(m * P, (m + 1) * P)
+            vc = slice(c * HALF, (c + 1) * HALF)
+            nc.tensor.matmul_mx(
+                out=acc[m][c][:],
+                lhsT=w_codes[g][:, mc].bitcast(FP8X4),
+                lhsT_scale=w_scales[g][:, mc],
+                rhs=codes[g][:, vc].bitcast(FP8X4),
+                rhs_scale=scales[g][:, vc],
+                start=(g == 0),
+                stop=(g == PASSES - 1),
+            )
+
+        def store(copy, m, c):
+            copy(out=res[m][c][:], in_=acc[m][c][:])
+            nc.sync.dma_start(out=out[m * P : (m + 1) * P, c * HALF : (c + 1) * HALF], in_=res[m][c][:])
+
+        sc, vc = nc.scalar.copy, nc.vector.tensor_copy
+        narrow = {}
+
+        def cast(engine_copy, l):
+            narrow[l] = keep.tile([P, T], BF16, name=f"narrow{l}", align_bytes=64)
+            engine_copy(out=narrow[l][:], in_=tables[l][:])
+
+        def scalar_gather(l, v0, v1):
+            g, j = divmod(l, PACK)
+            c0 = l * V // 16
+            nc.scalar.activation(
+                grouped[g][:, v0:v1, j],
+                narrow[l][:].indirect(offsets[:, c0 + v0 // 16 : c0 + v1 // 16]),
+                COPY,
+            )
+
+        def vector_gather(l, v0, v1):
+            g, j = divmod(l, PACK)
+            c0 = l * V // 16
+            nc.vector.tensor_copy(
+                grouped[g][:, v0:v1, j],
+                tables[l][:].indirect(offsets[:, c0 + v0 // 16 : c0 + v1 // 16]),
+            )
+
+        cast(vc, 0)
+        scalar_gather(0, 0, V)
+        vector_gather(2, 0, V)
+        cast(vc, 1)
+        scalar_gather(1, 0, V)
+        vector_gather(3, 0, V)
+        interleave_w(sc, 0)
+        interleave_w(sc, 1)
+        quantize(0, 0, V)
+        cast(vc, 4)
+        scalar_gather(4, 0, V)
+        quantize_w(0)
+        for m in range(2):
+            for c in range(2):
+                multiply(0, m, c)
+        cast(vc, 5)
+        scalar_gather(5, 0, V)
+        quantize_w(1)
+        vector_gather(6, 0, V)
+        vector_gather(7, 0, HALF)
+        vector_gather(7, HALF, V)
+        quantize(1, 0, HALF)
+        quantize(1, HALF, V)
+        for c in range(2):
+            for m in range(2):
+                multiply(1, m, c)
+        store(sc, 0, 0)
+        store(vc, 1, 0)
+        store(sc, 0, 1)
+        store(vc, 1, 1)

@@ -36,11 +36,11 @@ def tile_picked_grid_lin_none_sub_l_kernel(tc, xT, w, offs, out):
         nc.scalar.activation(warm_out[:], warm[:], COPY)
 
         tables = {}
-        w_raw = []
+        w_raw = {}
 
         def load_level(l):
             g, j = divmod(l, PACK)
-            table = keep.tile([P, T], F32, name=f"table{l}", align_bytes=64)
+            table = keep.tile([P, T], F32, name=f"table{l}", tag="table4" if l == 4 else f"table{l}", align_bytes=64)
             rows = xT[g * K_PASS : (g + 1) * K_PASS, :].rearrange("(p j) t -> p j t", j=PACK)
             nc.sync.dma_start(out=table[:], in_=rows[:, j, :])
             tables[l] = table
@@ -48,22 +48,22 @@ def tile_picked_grid_lin_none_sub_l_kernel(tc, xT, w, offs, out):
         def load_w(g):
             raw = keep.tile([P, PACK, N], F32, name=f"w_raw{g}", align_bytes=64)
             nc.sync.dma_start(out=raw[:], in_=w[g * K_PASS : (g + 1) * K_PASS, :].rearrange("(p j) n -> p j n", j=PACK))
-            w_raw.append(raw)
+            w_raw[g] = raw
 
         load_level(0)
         load_level(2)
         load_level(1)
         load_level(3)
-        load_w(0)
-        load_w(1)
         load_level(4)
-        load_level(5)
         load_level(6)
+        load_w(0)
+        load_level(5)
         load_level(7)
+        load_w(1)
 
         picked = [keep.tile([P, PACK, V], F32, name=f"picked{g}", align_bytes=64) for g in range(PASSES)]
         grouped = [keep.tile([P, V, PACK], BF16, name=f"grouped{g}", align_bytes=64) for g in range(PASSES)]
-        codes = [keep.tile([P, V], U32, name=f"codes{g}", align_bytes=64) for g in range(PASSES)]
+        codes = [None, keep.tile([P, V], U32, name="codes1", align_bytes=64)]
         scales = [keep.tile([P, V], U8, name=f"scales{g}", align_bytes=64) for g in range(PASSES)]
         w_grouped = [keep.tile([P, N, PACK], BF16, name=f"w_grouped{g}", align_bytes=64) for g in range(PASSES)]
         w_codes = [keep.tile([P, N], U32, name=f"w_codes{g}", align_bytes=64) for g in range(PASSES)]
@@ -92,14 +92,20 @@ def tile_picked_grid_lin_none_sub_l_kernel(tc, xT, w, offs, out):
                 in_=grouped[g][:, v0:v1, :].rearrange("p v j -> p (v j)"),
             )
 
-        def interleave_w(copy, g):
-            copy(out=w_grouped[g][:], in_=w_raw[g][:].rearrange("p j n -> p n j"))
+        def interleave_all(copy, dst, src):
+            copy(
+                out=dst.rearrange("p (c i) j -> p c j i", i=4),
+                in_=src.rearrange("p j (c i) -> p c j i", i=4),
+            )
 
-        def quantize_w(g):
+        def interleave_w(copy, g, n0, n1):
+            interleave_all(copy, w_grouped[g][:, n0:n1, :], w_raw[g][:, :, n0:n1])
+
+        def quantize_w(g, n0, n1):
             nc.vector.quantize_mx(
-                out=w_codes[g][:].bitcast(FP8X4),
-                scales=w_scales[g][:],
-                in_=w_grouped[g][:].rearrange("p n j -> p (n j)"),
+                out=w_codes[g][:, n0:n1].bitcast(FP8X4),
+                scales=w_scales[g][:, n0:n1],
+                in_=w_grouped[g][:, n0:n1, :].rearrange("p n j -> p (n j)"),
             )
 
         def multiply(g, m, c):
@@ -120,6 +126,7 @@ def tile_picked_grid_lin_none_sub_l_kernel(tc, xT, w, offs, out):
             nc.sync.dma_start(out=out[m * P : (m + 1) * P, c * HALF : (c + 1) * HALF], in_=res[m][c][:])
 
         sc, vc = nc.scalar.copy, nc.vector.tensor_copy
+
         narrow = {}
 
         def cast(engine_copy, l):
@@ -149,27 +156,30 @@ def tile_picked_grid_lin_none_sub_l_kernel(tc, xT, w, offs, out):
         cast(vc, 1)
         scalar_gather(1, 0, V)
         vector_gather(3, 0, V)
-        interleave_w(sc, 0)
-        interleave_w(sc, 1)
-        quantize(0, 0, V)
         cast(vc, 4)
         scalar_gather(4, 0, V)
-        quantize_w(0)
+        codes[0] = keep.tile([P, V], U32, name="codes0", tag="table4", align_bytes=64)
+        quantize(0, 0, V)
+        vector_gather(6, 0, V)
+        interleave_w(sc, 0, 0, N)
+        cast(vc, 5)
+        scalar_gather(5, 0, V)
+        quantize_w(0, 0, N)
         for m in range(2):
             for c in range(2):
                 multiply(0, m, c)
-        cast(vc, 5)
-        scalar_gather(5, 0, V)
-        quantize_w(1)
-        vector_gather(6, 0, V)
         vector_gather(7, 0, HALF)
+        interleave_w(sc, 1, 0, P)
+        interleave_w(sc, 1, P, N)
         vector_gather(7, HALF, V)
         quantize(1, 0, HALF)
+        quantize_w(1, 0, P)
         quantize(1, HALF, V)
-        for c in range(2):
-            for m in range(2):
+        quantize_w(1, P, N)
+        for m in range(2):
+            for c in range(2):
                 multiply(1, m, c)
         store(sc, 0, 0)
-        store(vc, 1, 0)
-        store(sc, 0, 1)
+        store(vc, 0, 1)
+        store(sc, 1, 0)
         store(vc, 1, 1)

@@ -28,7 +28,6 @@ def tile_picked_grid_lin_none_sub_l_kernel(tc, xT, w, offs, out):
         psum = ctx.enter_context(tc.psum_pool(name="psum", bufs=1))
 
         offsets = keep.tile([P, D * V // 16], U16, name="offsets")
-        nc.sync.dma_start(offsets[:], offs)
 
         warm = keep.tile([P, 1], F32, name="warm")
         warm_out = keep.tile([P, 1], F32, name="warm_out")
@@ -51,6 +50,7 @@ def tile_picked_grid_lin_none_sub_l_kernel(tc, xT, w, offs, out):
             w_raw[g] = raw
 
         load_level(0)
+        nc.sync.dma_start(offsets[:], offs)
         load_level(2)
         load_level(1)
         load_level(3)
@@ -168,6 +168,16 @@ def tile_picked_grid_lin_none_sub_l_kernel(tc, xT, w, offs, out):
         for m in range(2):
             for c in range(2):
                 multiply(0, m, c)
+        spin = psum.tile([P, V], F32, name="spin")
+        nc.tensor.matmul_mx(
+            out=spin[:],
+            lhsT=w_codes[0][:, 0:P].bitcast(FP8X4),
+            lhsT_scale=w_scales[0][:, 0:P],
+            rhs=codes[0][:].bitcast(FP8X4),
+            rhs_scale=scales[0][:],
+            start=True,
+            stop=True,
+        )
         vector_gather(7, 0, HALF)
         interleave_w(sc, 1, 0, P)
         interleave_w(sc, 1, P, N)

@@ -153,7 +153,7 @@ def tile_picked_grid_lin_none_sub_l_kernel(tc, xT, w, offs, out):
         cast(vc, 0)
         scalar_gather(0, 0, V)
         vector_gather(2, 0, V)
-        cast(vc, 1)
+        cast(sc, 1)
         scalar_gather(1, 0, V)
         vector_gather(3, 0, V)
         cast(vc, 4)
@@ -168,16 +168,6 @@ def tile_picked_grid_lin_none_sub_l_kernel(tc, xT, w, offs, out):
         for m in range(2):
             for c in range(2):
                 multiply(0, m, c)
-        spin = psum.tile([P, V], F32, name="spin")
-        nc.tensor.matmul_mx(
-            out=spin[:],
-            lhsT=w_codes[0][:, 0:P].bitcast(FP8X4),
-            lhsT_scale=w_scales[0][:, 0:P],
-            rhs=codes[0][:].bitcast(FP8X4),
-            rhs_scale=scales[0][:],
-            start=True,
-            stop=True,
-        )
         vector_gather(7, 0, HALF)
         interleave_w(sc, 1, 0, P)
         interleave_w(sc, 1, P, N)

from contextlib import ExitStack

import concourse.mybir as mybir

K, T, D, V, N = 1024, 1024, 8, 512, 256
FLOPS = 2 * K * N * V

F32 = mybir.dt.float32
BF16 = mybir.dt.bfloat16
U32 = mybir.dt.uint32
U16 = mybir.dt.uint16
U8 = mybir.dt.uint8
FP8X4 = mybir.dt.float8_e4m3fn_x4

COPY = mybir.ActivationFunctionType.Copy

P = 128
PACK = 4
K_PASS = P * PACK
PASSES = K // K_PASS
HALF = V // 2


def tile_picked_grid_lin_none_sub_l_kernel(tc, xT, w, offs, out):
    nc = tc.nc
    with ExitStack() as ctx:
        keep = ctx.enter_context(tc.tile_pool(name="keep", bufs=1))
        psum = ctx.enter_context(tc.psum_pool(name="psum", bufs=1))

        offsets = keep.tile([P, D * V // 16], U16, name="offsets")

        warm = keep.tile([P, 1], F32, name="warm")
        warm_out = keep.tile([P, 1], F32, name="warm_out")
        nc.vector.memset(warm[:], 0.0)
        nc.scalar.activation(warm_out[:], warm[:], COPY)

        tables = {}
        w_raw = {}

        def load_level(l):
            g, j = divmod(l, PACK)
            table = keep.tile([P, T], F32, name=f"table{l}", tag="table4" if l == 4 else f"table{l}", align_bytes=64)
            rows = xT[g * K_PASS : (g + 1) * K_PASS, :].rearrange("(p j) t -> p j t", j=PACK)
            nc.sync.dma_start(out=table[:], in_=rows[:, j, :])
            tables[l] = table

        def load_w(g):
            raw = keep.tile([P, PACK, N], F32, name=f"w_raw{g}", align_bytes=64)
            nc.sync.dma_start(out=raw[:], in_=w[g * K_PASS : (g + 1) * K_PASS, :].rearrange("(p j) n -> p j n", j=PACK))
            w_raw[g] = raw

        load_level(0)
        nc.sync.dma_start(offsets[:], offs)
        load_level(2)
        load_level(1)
        load_level(3)
        load_level(4)
        load_level(6)
        load_w(0)
        load_level(5)
        load_level(7)
        load_w(1)

        picked = [keep.tile([P, PACK, V], F32, name=f"picked{g}", align_bytes=64) for g in range(PASSES)]
        grouped = [keep.tile([P, V, PACK], BF16, name=f"grouped{g}", align_bytes=64) for g in range(PASSES)]
        codes = [None, keep.tile([P, V], U32, name="codes1", align_bytes=64)]
        scales = [keep.tile([P, V], U8, name=f"scales{g}", align_bytes=64) for g in range(PASSES)]
        w_grouped = [keep.tile([P, N, PACK], BF16, name=f"w_grouped{g}", align_bytes=64) for g in range(PASSES)]
        w_codes = [keep.tile([P, N], U32, name=f"w_codes{g}", align_bytes=64) for g in range(PASSES)]
        w_scales = [keep.tile([P, N], U8, name=f"w_scales{g}", align_bytes=64) for g in range(PASSES)]
        acc = [[psum.tile([P, HALF], F32, name=f"acc{m}{c}") for c in range(2)] for m in range(2)]
        res = [[keep.tile([P, HALF], F32, name=f"res{m}{c}", align_bytes=64) for c in range(2)] for m in range(2)]

        def gather(l, v0, v1):
            g, j = divmod(l, PACK)
            c0 = l * V // 16
            nc.vector.tensor_copy(
                picked[g][:, j, v0:v1],
                tables[l][:].indirect(offsets[:, c0 + v0 // 16 : c0 + v1 // 16]),
            )

        def interleave(copy, g, j0, j1, v0, v1):
            copy(
                out=grouped[g][:, v0:v1, j0:j1],
                in_=picked[g][:, j0:j1, v0:v1].rearrange("p j v -> p v j"),
            )

        def quantize(g, v0, v1):
            nc.vector.quantize_mx(
                out=codes[g][:, v0:v1].bitcast(FP8X4),
                scales=scales[g][:, v0:v1],
                in_=grouped[g][:, v0:v1, :].rearrange("p v j -> p (v j)"),
            )

        def interleave_all(copy, dst, src):
            copy(
                out=dst.rearrange("p (c i) j -> p c j i", i=4),
                in_=src.rearrange("p j (c i) -> p c j i", i=4),
            )

        def interleave_w(copy, g, n0, n1):
            interleave_all(copy, w_grouped[g][:, n0:n1, :], w_raw[g][:, :, n0:n1])

        def quantize_w(g, n0, n1):
            nc.vector.quantize_mx(
                out=w_codes[g][:, n0:n1].bitcast(FP8X4),
                scales=w_scales[g][:, n0:n1],
                in_=w_grouped[g][:, n0:n1, :].rearrange("p n j -> p (n j)"),
            )

        def multiply(g, m, c):
            mc = slice(m * P, (m + 1) * P)
            vc = slice(c * HALF, (c + 1) * HALF)
            nc.tensor.matmul_mx(
                out=acc[m][c][:],
                lhsT=w_codes[g][:, mc].bitcast(FP8X4),
                lhsT_scale=w_scales[g][:, mc],
                rhs=codes[g][:, vc].bitcast(FP8X4),
                rhs_scale=scales[g][:, vc],
                start=(g == 0),
                stop=(g == PASSES - 1),
            )

        def store(copy, m, c):
            copy(out=res[m][c][:], in_=acc[m][c][:])
            nc.sync.dma_start(out=out[m * P : (m + 1) * P, c * HALF : (c + 1) * HALF], in_=res[m][c][:])

        sc, vc = nc.scalar.copy, nc.vector.tensor_copy

        narrow = {}

        def cast(engine_copy, l):
            narrow[l] = keep.tile([P, T], BF16, name=f"narrow{l}", align_bytes=64)
            engine_copy(out=narrow[l][:], in_=tables[l][:])

        def scalar_gather(l, v0, v1):
            g, j = divmod(l, PACK)
            c0 = l * V // 16
            nc.scalar.activation(
                grouped[g][:, v0:v1, j],
                narrow[l][:].indirect(offsets[:, c0 + v0 // 16 : c0 + v1 // 16]),
                COPY,
            )

        def vector_gather(l, v0, v1):
            g, j = divmod(l, PACK)
            c0 = l * V // 16
            nc.vector.tensor_copy(
                grouped[g][:, v0:v1, j],
                tables[l][:].indirect(offsets[:, c0 + v0 // 16 : c0 + v1 // 16]),
            )

        cast(vc, 0)
        scalar_gather(0, 0, V)
        vector_gather(2, 0, V)
        cast(sc, 1)
        scalar_gather(1, 0, V)
        vector_gather(3, 0, V)
        cast(vc, 4)
        scalar_gather(4, 0, V)
        codes[0] = keep.tile([P, V], U32, name="codes0", tag="table4", align_bytes=64)
        quantize(0, 0, V)
        vector_gather(6, 0, V)
        interleave_w(sc, 0, 0, N)
        cast(vc, 5)
        scalar_gather(5, 0, V)
        quantize_w(0, 0, N)
        for m in range(2):
            for c in range(2):
                multiply(0, m, c)
        vector_gather(7, 0, HALF)
        interleave_w(sc, 1, 0, P)
        interleave_w(sc, 1, P, N)
        vector_gather(7, HALF, V)
        quantize(1, 0, HALF)
        quantize_w(1, 0, P)
        quantize(1, HALF, V)
        quantize_w(1, P, N)
        for m in range(2):
            for c in range(2):
                multiply(1, m, c)
        store(sc, 0, 0)
        store(vc, 0, 1)
        store(sc, 1, 0)
        store(vc, 1, 1)
